import numpy as np
import ml_dtypes


def mxq(x, axis, fmt="e4m3"):
    dtype, down = {"e4m3": (ml_dtypes.float8_e4m3fn, 7), "e5m2": (ml_dtypes.float8_e5m2, 14)}[fmt]
    v = np.moveaxis(np.asarray(x, np.float32).astype(ml_dtypes.bfloat16).astype(np.float64), axis, -1)
    blocks = v.reshape(v.shape[:-1] + (-1, 32))
    amax = np.abs(blocks).max(-1, keepdims=True)
    byte = np.maximum(np.where(amax > 0, np.frexp(amax)[1] - 1 + 127, 0) - down, 1)
    scale = np.exp2(byte - 127.0)
    codes = (blocks / scale).astype(np.float32).astype(dtype).astype(np.float64)
    return np.moveaxis((codes * scale).reshape(v.shape), -1, axis)


WIDE = False


def mx_kscale(k):
    if not WIDE:
        return np.ones(k)
    levels = np.array([10, -10, 5, -5, 0])
    if k % 512:
        return np.exp2(np.random.permutation(np.resize(levels, k // 32))).repeat(32)
    a = np.empty((k // 512, 16))
    for p in range(k // 512):
        a[p, :8] = np.random.permutation(np.resize(levels, 8))
        for g in range(8):
            far = levels[np.abs(levels - a[p, g]) >= 10]
            a[p, g + 8] = far[np.random.randint(len(far))]
    return np.exp2(a.ravel()).repeat(32)


def f64(x):
    return np.asarray(x).astype(np.float64)


def striped(idx):
    return np.tile(idx.reshape(-1, 16).T, (8, 1)).astype(np.uint16)


def unstriped(offs):
    return offs[:16].T.reshape(-1).astype(np.int64)


def gelu(v):
    return 0.5 * v * (1.0 + np.tanh(np.sqrt(2.0 / np.pi) * (v + 0.044715 * v**3)))


K, T, D, S, V, R, N = 512, 4096, 4, 4096, 1024, 4, 128


def setup_inputs():
    n = np.random.standard_normal
    s = mx_kscale(K)[:, None]
    return {
        "xT": (n((K, T)) * s).astype(np.float32),
        "w": (n((D, K, N)) / np.sqrt(D * K) / s[None]).astype(np.float32),
        "b": (0.3 * n((N, 1))).astype(np.float32),
        "offs": striped(np.concatenate([R * np.arange(V) + np.random.randint(0, R, V) for _ in range(D)])),
    }


def reference(xT, w, b, offs):
    idx = unstriped(offs)
    xq = mxq(f64(xT)[:, idx], 0, "e4m3")
    wq = mxq(f64(w), 1, "e4m3")
    y = sum(wq[d].T @ xq[:, d * V:(d + 1) * V] for d in range(D))
    y = gelu(y + f64(b))
    return y

@@ -1,0 +1,127 @@
+from contextlib import ExitStack
+
+import concourse.mybir as mybir
+
+K, T, D, V, N = 512, 4096, 4, 1024, 128
+P = 128
+PACK = 4
+HALF = 512
+FLOPS = 2 * D * K * N * V
+
+F32 = mybir.dt.float32
+BF16 = mybir.dt.bfloat16
+U32 = mybir.dt.uint32
+U16 = mybir.dt.uint16
+U8 = mybir.dt.uint8
+FP8X4 = mybir.dt.float8_e4m3fn_x4
+GELU = mybir.ActivationFunctionType.Gelu_apprx_tanh
+
+CHUNKS = [(256, 256), (256, 256), (512, 512), (512, 512), (512, 512), (512, 448), (512, 448), (512, 448), (256, 192), (256, 128)]
+RANGES = [(0, 128), (128, 256), (256, 512), (512, 1024)]
+
+
+def tile_picked_deform_lin_gelu_def_e_kernel(tc, xT, w, b, offs, out):
+    nc = tc.nc
+    with ExitStack() as ctx:
+        keep = ctx.enter_context(tc.tile_pool(name="keep", bufs=1))
+        psum = ctx.enter_context(tc.psum_pool(name="psum", bufs=1))
+
+        lists = keep.tile([P, D * V // 16], U16, name="lists")
+        words = keep.tile([P, T], U32, name="words", align_bytes=64)
+        scales = keep.tile([P, T], U8, name="scales", align_bytes=64)
+        bias = keep.tile([P, 1], F32, name="bias")
+        warm = keep.tile([P, 1], F32, name="warm")
+        warm_out = keep.tile([P, 1], F32, name="warm_out")
+
+        nc.vector.memset(warm[:], 0.0)
+        nc.scalar.activation(warm_out[:], warm[:], GELU)
+        for q in range(4):
+            nc.gpsimd.memset(scales[:, q * 1024 : (q + 1) * 1024], 0)
+
+        raws = []
+        x_view = xT.rearrange("(p j) t -> p j t", j=PACK)
+        start = 0
+        for i, (width, share) in enumerate(CHUNKS):
+            raw = keep.tile([P, PACK, width], F32, name="raw%d" % i)
+            nc.sync.dma_start(out=raw[:], in_=x_view[:, :, start : start + width])
+            raws.append((start, raw))
+            start += width
+            if i == 1:
+                nc.sync.dma_start(lists[:], offs)
+        w_raw = []
+        for h in range(2):
+            wr = keep.tile([P, 2, PACK, N], F32, name="w_raw%d" % h)
+            nc.sync.dma_start(out=wr[:], in_=w[2 * h : 2 * h + 2].rearrange("d (p j) m -> p d j m", j=PACK))
+            w_raw.append(wr)
+        nc.sync.dma_start(out=bias[:], in_=b)
+
+        picked = {}
+
+        def interleave(copy, dst, src):
+            copy(
+                out=dst.rearrange("p (c i) t -> p c t i", i=4),
+                in_=src.rearrange("p t (c i) -> p c t i", i=4),
+            )
+
+        def gather(lo, hi, t):
+            h, c = divmod(lo, HALF)
+            if c == 0:
+                tag = "shared%d" % (t - 2) if h == 1 and t >= 2 else "pw%d_%d" % (h, t)
+                pw = keep.tile([P, HALF], U32, name="pw%d_%d" % (h, t), tag=tag, align_bytes=64)
+                ps = keep.tile([P, HALF], U8, name="ps%d_%d" % (h, t), align_bytes=64)
+                picked[h, t] = (pw, ps)
+            pw, ps = picked[h, t]
+            dst = slice(c, c + hi - lo)
+            part = lists[:, (t * V + lo) // 16 : (t * V + hi) // 16]
+            nc.vector.tensor_copy(pw[:, dst], words[:, 0 : 4 * hi].indirect(part))
+            nc.vector.tensor_copy(ps[:, dst], scales[:, 0 : 4 * hi].indirect(part))
+
+        ranges = list(RANGES)
+        for i, (width, share) in enumerate(CHUNKS):
+            start, raw = raws[i]
+            grouped = keep.tile([P, width, PACK], BF16, name="grouped%d" % i, align_bytes=64)
+            interleave(nc.scalar.copy, grouped[:, 0:share, :], raw[:, :, 0:share])
+            if share < width:
+                interleave(nc.vector.tensor_copy, grouped[:, share:width, :], raw[:, :, share:width])
+            nc.vector.quantize_mx(
+                out=words[:, start : start + width].bitcast(FP8X4),
+                scales=scales[:, start : start + width],
+                in_=grouped[:].rearrange("p c t -> p (c t)"),
+            )
+            while ranges and 4 * ranges[0][1] <= start + width and ranges[0][1] < V:
+                lo, hi = ranges.pop(0)
+                for t in range(D):
+                    gather(lo, hi, t)
+
+        w_words = keep.tile([P, D * N], U32, name="w_words", align_bytes=64)
+        w_scales = keep.tile([P, D * N], U8, name="w_scales", align_bytes=64)
+        for g in range(2):
+            w_grouped = keep.tile([P, 2, N, PACK], BF16, name="w_grouped%d" % g, tag="shared%d" % g, align_bytes=64)
+            for t in range(2):
+                interleave(nc.scalar.copy, w_grouped[:, t], w_raw[g][:, t])
+            nc.vector.quantize_mx(
+                out=w_words[:, g * 2 * N : (g + 1) * 2 * N].bitcast(FP8X4),
+                scales=w_scales[:, g * 2 * N : (g + 1) * 2 * N],
+                in_=w_grouped[:].rearrange("p d m t -> p (d m t)"),
+            )
+        lo, hi = ranges.pop(0)
+        for t in range(D):
+            gather(lo, hi, t)
+
+        for h in range(2):
+            acc = psum.tile([N, HALF], F32, name="acc%d" % h)
+            for t in range(D):
+                cols = slice(t * N, (t + 1) * N)
+                nc.tensor.matmul_mx(
+                    out=acc[:],
+                    lhsT=w_words[:, cols].bitcast(FP8X4),
+                    lhsT_scale=w_scales[:, cols],
+                    rhs=picked[h, t][0][:].bitcast(FP8X4),
+                    rhs_scale=picked[h, t][1][:],
+                    start=(t == 0),
+                    stop=(t == D - 1),
+                )
+            for q in range(2):
+                result = keep.tile([N, HALF // 2], F32, name="result%d_%d" % (h, q))
+                nc.scalar.activation(result[:], acc[:, q * 256 : (q + 1) * 256], GELU, bias=bias[:])
+                nc.sync.dma_start(out=out[:, h * HALF + q * 256 : h * HALF + (q + 1) * 256], in_=result[:])

@@ -10,13 +10,14 @@ FLOPS = 2 * D * K * N * V
 
 F32 = mybir.dt.float32
 BF16 = mybir.dt.bfloat16
+I32 = mybir.dt.int32
 U32 = mybir.dt.uint32
 U16 = mybir.dt.uint16
 U8 = mybir.dt.uint8
 FP8X4 = mybir.dt.float8_e4m3fn_x4
 GELU = mybir.ActivationFunctionType.Gelu_apprx_tanh
 
-CHUNKS = [(256, 256), (256, 256), (512, 512), (512, 512), (512, 512), (512, 448), (512, 448), (512, 448), (256, 192), (256, 128)]
+CHUNKS = [(256, 256), (256, 128), (512, 384), (512, 512), (512, 320), (512, 512), (512, 512), (512, 288), (256, 256), (256, 128)]
 RANGES = [(0, 128), (128, 256), (256, 512), (512, 1024)]
 
 
@@ -24,6 +25,7 @@ def tile_picked_deform_lin_gelu_def_e_kernel(tc, xT, w, b, offs, out):
     nc = tc.nc
     with ExitStack() as ctx:
         keep = ctx.enter_context(tc.tile_pool(name="keep", bufs=1))
+        late = ctx.enter_context(tc.tile_pool(name="late", bufs=1))
         psum = ctx.enter_context(tc.psum_pool(name="psum", bufs=1))
 
         lists = keep.tile([P, D * V // 16], U16, name="lists")
@@ -35,8 +37,7 @@ def tile_picked_deform_lin_gelu_def_e_kernel(tc, xT, w, b, offs, out):
 
         nc.vector.memset(warm[:], 0.0)
         nc.scalar.activation(warm_out[:], warm[:], GELU)
-        for q in range(4):
-            nc.gpsimd.memset(scales[:, q * 1024 : (q + 1) * 1024], 0)
+        nc.gpsimd.memset(scales[:].bitcast(I32), 0)
 
         raws = []
         x_view = xT.rearrange("(p j) t -> p j t", j=PACK)
@@ -57,18 +58,21 @@ def tile_picked_deform_lin_gelu_def_e_kernel(tc, xT, w, b, offs, out):
 
         picked = {}
 
-        def interleave(copy, dst, src):
+        def interleave(copy, run, dst, src):
             copy(
-                out=dst.rearrange("p (c i) t -> p c t i", i=4),
-                in_=src.rearrange("p t (c i) -> p c t i", i=4),
+                out=dst.rearrange("p (c i) t -> p c t i", i=run),
+                in_=src.rearrange("p t (c i) -> p c t i", i=run),
             )
 
         def gather(lo, hi, t):
             h, c = divmod(lo, HALF)
             if c == 0:
-                tag = "shared%d" % (t - 2) if h == 1 and t >= 2 else "pw%d_%d" % (h, t)
-                pw = keep.tile([P, HALF], U32, name="pw%d_%d" % (h, t), tag=tag, align_bytes=64)
-                ps = keep.tile([P, HALF], U8, name="ps%d_%d" % (h, t), align_bytes=64)
+                if h == 1 and t >= 2:
+                    ps = late.tile([P, HALF], U8, name="ps%d_%d" % (h, t), align_bytes=64, offset=(t - 2) * HALF)
+                    pw = late.tile([P, HALF], U32, name="pw%d_%d" % (h, t), align_bytes=64, offset=(4 * t - 6) * HALF)
+                else:
+                    pw = keep.tile([P, HALF], U32, name="pw%d_%d" % (h, t), align_bytes=64)
+                    ps = keep.tile([P, HALF], U8, name="ps%d_%d" % (h, t), align_bytes=64)
                 picked[h, t] = (pw, ps)
             pw, ps = picked[h, t]
             dst = slice(c, c + hi - lo)
@@ -80,9 +84,9 @@ def tile_picked_deform_lin_gelu_def_e_kernel(tc, xT, w, b, offs, out):
         for i, (width, share) in enumerate(CHUNKS):
             start, raw = raws[i]
             grouped = keep.tile([P, width, PACK], BF16, name="grouped%d" % i, align_bytes=64)
-            interleave(nc.scalar.copy, grouped[:, 0:share, :], raw[:, :, 0:share])
+            interleave(nc.scalar.copy, 2, grouped[:, 0:share, :], raw[:, :, 0:share])
             if share < width:
-                interleave(nc.vector.tensor_copy, grouped[:, share:width, :], raw[:, :, share:width])
+                interleave(nc.vector.tensor_copy, 4, grouped[:, share:width, :], raw[:, :, share:width])
             nc.vector.quantize_mx(
                 out=words[:, start : start + width].bitcast(FP8X4),
                 scales=scales[:, start : start + width],
@@ -95,15 +99,14 @@ def tile_picked_deform_lin_gelu_def_e_kernel(tc, xT, w, b, offs, out):
 
         w_words = keep.tile([P, D * N], U32, name="w_words", align_bytes=64)
         w_scales = keep.tile([P, D * N], U8, name="w_scales", align_bytes=64)
-        for g in range(2):
-            w_grouped = keep.tile([P, 2, N, PACK], BF16, name="w_grouped%d" % g, tag="shared%d" % g, align_bytes=64)
-            for t in range(2):
-                interleave(nc.scalar.copy, w_grouped[:, t], w_raw[g][:, t])
-            nc.vector.quantize_mx(
-                out=w_words[:, g * 2 * N : (g + 1) * 2 * N].bitcast(FP8X4),
-                scales=w_scales[:, g * 2 * N : (g + 1) * 2 * N],
-                in_=w_grouped[:].rearrange("p d m t -> p (d m t)"),
-            )
+        w_grouped = late.tile([P, D, N, PACK], BF16, name="w_grouped", align_bytes=64, offset=0)
+        for t in range(D):
+            interleave(nc.scalar.copy, 2, w_grouped[:, t], w_raw[t // 2][:, t % 2])
+        nc.vector.quantize_mx(
+            out=w_words[:].bitcast(FP8X4),
+            scales=w_scales[:],
+            in_=w_grouped[:].rearrange("p d m t -> p (d m t)"),
+        )
         lo, hi = ranges.pop(0)
         for t in range(D):
             gather(lo, hi, t)

@@ -17,7 +17,7 @@ U8 = mybir.dt.uint8
 FP8X4 = mybir.dt.float8_e4m3fn_x4
 GELU = mybir.ActivationFunctionType.Gelu_apprx_tanh
 
-CHUNKS = [(256, 256), (256, 128), (512, 384), (512, 512), (512, 320), (512, 512), (512, 512), (512, 288), (256, 256), (256, 128)]
+CHUNKS = [(256, 128), (256, 64), (256, 256), (256, 256), (512, 512), (512, 320), (512, 448), (512, 512), (512, 512), (256, 0), (256, 256)]
 RANGES = [(0, 128), (128, 256), (256, 512), (512, 1024)]
 
 
@@ -51,7 +51,10 @@ def tile_picked_deform_lin_gelu_def_e_kernel(tc, xT, w, b, offs, out):
                 nc.sync.dma_start(lists[:], offs)
         w_raw = []
         for h in range(2):
-            wr = keep.tile([P, 2, PACK, N], F32, name="w_raw%d" % h)
+            if h == 0:
+                wr = keep.tile([P, 2, PACK, N], F32, name="w_raw0")
+            else:
+                wr = late.tile([P, 2, PACK, N], F32, name="w_raw1", align_bytes=64, offset=0)
             nc.sync.dma_start(out=wr[:], in_=w[2 * h : 2 * h + 2].rearrange("d (p j) m -> p d j m", j=PACK))
             w_raw.append(wr)
         nc.sync.dma_start(out=bias[:], in_=b)
@@ -67,12 +70,14 @@ def tile_picked_deform_lin_gelu_def_e_kernel(tc, xT, w, b, offs, out):
         def gather(lo, hi, t):
             h, c = divmod(lo, HALF)
             if c == 0:
+                if h == 1 and t >= 1:
+                    ps = late.tile([P, HALF], U8, name="ps%d_%d" % (h, t), align_bytes=64, offset=(t - 1) * HALF)
+                else:
+                    ps = keep.tile([P, HALF], U8, name="ps%d_%d" % (h, t), align_bytes=64)
                 if h == 1 and t >= 2:
-                    ps = late.tile([P, HALF], U8, name="ps%d_%d" % (h, t), align_bytes=64, offset=(t - 2) * HALF)
-                    pw = late.tile([P, HALF], U32, name="pw%d_%d" % (h, t), align_bytes=64, offset=(4 * t - 6) * HALF)
+                    pw = late.tile([P, HALF], U32, name="pw%d_%d" % (h, t), align_bytes=64, offset=(4 * t - 5) * HALF)
                 else:
                     pw = keep.tile([P, HALF], U32, name="pw%d_%d" % (h, t), align_bytes=64)
-                    ps = keep.tile([P, HALF], U8, name="ps%d_%d" % (h, t), align_bytes=64)
                 picked[h, t] = (pw, ps)
             pw, ps = picked[h, t]
             dst = slice(c, c + hi - lo)
@@ -84,7 +89,8 @@ def tile_picked_deform_lin_gelu_def_e_kernel(tc, xT, w, b, offs, out):
         for i, (width, share) in enumerate(CHUNKS):
             start, raw = raws[i]
             grouped = keep.tile([P, width, PACK], BF16, name="grouped%d" % i, align_bytes=64)
-            interleave(nc.scalar.copy, 2, grouped[:, 0:share, :], raw[:, :, 0:share])
+            if share > 0:
+                interleave(nc.scalar.copy, 2, grouped[:, 0:share, :], raw[:, :, 0:share])
             if share < width:
                 interleave(nc.vector.tensor_copy, 4, grouped[:, share:width, :], raw[:, :, share:width])
             nc.vector.quantize_mx(
@@ -99,7 +105,7 @@ def tile_picked_deform_lin_gelu_def_e_kernel(tc, xT, w, b, offs, out):
 
         w_words = keep.tile([P, D * N], U32, name="w_words", align_bytes=64)
         w_scales = keep.tile([P, D * N], U8, name="w_scales", align_bytes=64)
-        w_grouped = late.tile([P, D, N, PACK], BF16, name="w_grouped", align_bytes=64, offset=0)
+        w_grouped = keep.tile([P, D, N, PACK], BF16, name="w_grouped", align_bytes=64)
         for t in range(D):
             interleave(nc.scalar.copy, 2, w_grouped[:, t], w_raw[t // 2][:, t % 2])
         nc.vector.quantize_mx(

@@ -17,8 +17,8 @@ U8 = mybir.dt.uint8
 FP8X4 = mybir.dt.float8_e4m3fn_x4
 GELU = mybir.ActivationFunctionType.Gelu_apprx_tanh
 
-CHUNKS = [(256, 128), (256, 64), (256, 256), (256, 256), (512, 512), (512, 320), (512, 448), (512, 512), (512, 512), (256, 0), (256, 256)]
-RANGES = [(0, 128), (128, 256), (256, 512), (512, 1024)]
+CHUNKS = [(1024, 384), (512, 512), (512, 512), (512, 512), (512, 512), (512, 384), (256, 256), (256, 128)]
+RANGES = [(0, 256), (256, 512), (512, 1024)]
 
 
 def tile_picked_deform_lin_gelu_def_e_kernel(tc, xT, w, b, offs, out):
@@ -47,7 +47,7 @@ def tile_picked_deform_lin_gelu_def_e_kernel(tc, xT, w, b, offs, out):
             nc.sync.dma_start(out=raw[:], in_=x_view[:, :, start : start + width])
             raws.append((start, raw))
             start += width
-            if i == 1:
+            if i == 0:
                 nc.sync.dma_start(lists[:], offs)
         w_raw = []
         for h in range(2):
@@ -70,7 +70,7 @@ def tile_picked_deform_lin_gelu_def_e_kernel(tc, xT, w, b, offs, out):
         def gather(lo, hi, t):
             h, c = divmod(lo, HALF)
             if c == 0:
-                if h == 1 and t >= 1:
+                if h == 1 and t >= 2:
                     ps = late.tile([P, HALF], U8, name="ps%d_%d" % (h, t), align_bytes=64, offset=(t - 1) * HALF)
                 else:
                     ps = keep.tile([P, HALF], U8, name="ps%d_%d" % (h, t), align_bytes=64)

@@ -32,11 +32,7 @@ def tile_picked_deform_lin_gelu_def_e_kernel(tc, xT, w, b, offs, out):
         words = keep.tile([P, T], U32, name="words", align_bytes=64)
         scales = keep.tile([P, T], U8, name="scales", align_bytes=64)
         bias = keep.tile([P, 1], F32, name="bias")
-        warm = keep.tile([P, 1], F32, name="warm")
-        warm_out = keep.tile([P, 1], F32, name="warm_out")
 
-        nc.vector.memset(warm[:], 0.0)
-        nc.scalar.activation(warm_out[:], warm[:], GELU)
         nc.gpsimd.memset(scales[:].bitcast(I32), 0)
 
         raws = []

@@ -17,7 +17,7 @@ U8 = mybir.dt.uint8
 FP8X4 = mybir.dt.float8_e4m3fn_x4
 GELU = mybir.ActivationFunctionType.Gelu_apprx_tanh
 
-CHUNKS = [(1024, 384), (512, 512), (512, 512), (512, 512), (512, 512), (512, 384), (256, 256), (256, 128)]
+CHUNKS = [(1024, 320), (512, 512), (512, 512), (512, 512), (512, 512), (512, 384), (256, 256), (256, 128)]
 RANGES = [(0, 256), (256, 512), (512, 1024)]
 
 

@@ -5,7 +5,6 @@ import concourse.mybir as mybir
 K, T, D, V, N = 512, 4096, 4, 1024, 128
 P = 128
 PACK = 4
-HALF = 512
 FLOPS = 2 * D * K * N * V
 
 F32 = mybir.dt.float32
@@ -17,8 +16,9 @@ U8 = mybir.dt.uint8
 FP8X4 = mybir.dt.float8_e4m3fn_x4
 GELU = mybir.ActivationFunctionType.Gelu_apprx_tanh
 
-CHUNKS = [(1024, 320), (512, 512), (512, 512), (512, 512), (512, 512), (512, 384), (256, 256), (256, 128)]
-RANGES = [(0, 256), (256, 512), (512, 1024)]
+CHUNKS = [(512, 192), (512, 384), (512, 512), (512, 320), (512, 512), (512, 512), (512, 512), (256, 256), (256, 128)]
+LOW = [(0, 128), (128, 256), (256, 512)]
+HALF, QUARTER = V // 2, V // 4
 
 
 def tile_picked_deform_lin_gelu_def_e_kernel(tc, xT, w, b, offs, out):
@@ -46,16 +46,12 @@ def tile_picked_deform_lin_gelu_def_e_kernel(tc, xT, w, b, offs, out):
             if i == 0:
                 nc.sync.dma_start(lists[:], offs)
         w_raw = []
+        half_bytes = 2 * PACK * N * 4
         for h in range(2):
-            if h == 0:
-                wr = keep.tile([P, 2, PACK, N], F32, name="w_raw0")
-            else:
-                wr = late.tile([P, 2, PACK, N], F32, name="w_raw1", align_bytes=64, offset=0)
+            wr = late.tile([P, 2, PACK, N], F32, name="w_raw%d" % h, align_bytes=64, offset=h * half_bytes)
             nc.sync.dma_start(out=wr[:], in_=w[2 * h : 2 * h + 2].rearrange("d (p j) m -> p d j m", j=PACK))
             w_raw.append(wr)
         nc.sync.dma_start(out=bias[:], in_=b)
-
-        picked = {}
 
         def interleave(copy, run, dst, src):
             copy(
@@ -63,25 +59,13 @@ def tile_picked_deform_lin_gelu_def_e_kernel(tc, xT, w, b, offs, out):
                 in_=src.rearrange("p t (c i) -> p c t i", i=run),
             )
 
-        def gather(lo, hi, t):
-            h, c = divmod(lo, HALF)
-            if c == 0:
-                if h == 1 and t >= 2:
-                    ps = late.tile([P, HALF], U8, name="ps%d_%d" % (h, t), align_bytes=64, offset=(t - 1) * HALF)
-                else:
-                    ps = keep.tile([P, HALF], U8, name="ps%d_%d" % (h, t), align_bytes=64)
-                if h == 1 and t >= 2:
-                    pw = late.tile([P, HALF], U32, name="pw%d_%d" % (h, t), align_bytes=64, offset=(4 * t - 5) * HALF)
-                else:
-                    pw = keep.tile([P, HALF], U32, name="pw%d_%d" % (h, t), align_bytes=64)
-                picked[h, t] = (pw, ps)
-            pw, ps = picked[h, t]
-            dst = slice(c, c + hi - lo)
-            part = lists[:, (t * V + lo) // 16 : (t * V + hi) // 16]
-            nc.vector.tensor_copy(pw[:, dst], words[:, 0 : 4 * hi].indirect(part))
-            nc.vector.tensor_copy(ps[:, dst], scales[:, 0 : 4 * hi].indirect(part))
+        def gather(dst, window, t, lo, hi):
+            nc.vector.tensor_copy(dst, window.indirect(lists[:, (t * V + lo) // 16 : (t * V + hi) // 16]))
 
-        ranges = list(RANGES)
+        low_words = [keep.tile([P, HALF], U32, name="low_words%d" % t, align_bytes=64) for t in range(D)]
+        low_bytes = [keep.tile([P, HALF], U8, name="low_bytes%d" % t, align_bytes=64) for t in range(D)]
+        mid_words = [keep.tile([P, QUARTER], U32, name="mid_words%d" % t, align_bytes=64) for t in range(D)]
+
         for i, (width, share) in enumerate(CHUNKS):
             start, raw = raws[i]
             grouped = keep.tile([P, width, PACK], BF16, name="grouped%d" % i, align_bytes=64)
@@ -94,39 +78,72 @@ def tile_picked_deform_lin_gelu_def_e_kernel(tc, xT, w, b, offs, out):
                 scales=scales[:, start : start + width],
                 in_=grouped[:].rearrange("p c t -> p (c t)"),
             )
-            while ranges and 4 * ranges[0][1] <= start + width and ranges[0][1] < V:
-                lo, hi = ranges.pop(0)
+            done = start + width
+            for lo, hi in LOW:
+                if PACK * hi == done:
+                    for t in range(D):
+                        gather(low_words[t][:, lo:hi], words[:, 0:done], t, lo, hi)
+                        gather(low_bytes[t][:, lo:hi], scales[:, 0:done], t, lo, hi)
+            if done == PACK * (HALF + QUARTER):
                 for t in range(D):
-                    gather(lo, hi, t)
+                    gather(mid_words[t][:], words[:], t, HALF, HALF + QUARTER)
 
         w_words = keep.tile([P, D * N], U32, name="w_words", align_bytes=64)
         w_scales = keep.tile([P, D * N], U8, name="w_scales", align_bytes=64)
         w_grouped = keep.tile([P, D, N, PACK], BF16, name="w_grouped", align_bytes=64)
-        for t in range(D):
-            interleave(nc.scalar.copy, 2, w_grouped[:, t], w_raw[t // 2][:, t % 2])
-        nc.vector.quantize_mx(
-            out=w_words[:].bitcast(FP8X4),
-            scales=w_scales[:],
-            in_=w_grouped[:].rearrange("p d m t -> p (d m t)"),
-        )
-        lo, hi = ranges.pop(0)
-        for t in range(D):
-            gather(lo, hi, t)
 
-        for h in range(2):
-            acc = psum.tile([N, HALF], F32, name="acc%d" % h)
-            for t in range(D):
-                cols = slice(t * N, (t + 1) * N)
+        def quantise_w(h):
+            for t in range(2 * h, 2 * h + 2):
+                interleave(nc.scalar.copy, 2, w_grouped[:, t], w_raw[h][:, t % 2])
+            cols = slice(2 * h * N, (2 * h + 2) * N)
+            nc.vector.quantize_mx(
+                out=w_words[:, cols].bitcast(FP8X4),
+                scales=w_scales[:, cols],
+                in_=w_grouped[:, 2 * h : 2 * h + 2].rearrange("p d m t -> p (d m t)"),
+            )
+
+        top_words, top_bytes = [], []
+        for t in range(D):
+            if t == 0:
+                tw = keep.tile([P, QUARTER], U32, name="top_words0", align_bytes=64)
+                tb = keep.tile([P, HALF], U8, name="top_bytes0", align_bytes=64)
+            else:
+                base = (t // 2) * half_bytes + (t % 2) * 2048
+                tw = late.tile([P, QUARTER], U32, name="top_words%d" % t, align_bytes=64, offset=base)
+                tb = late.tile([P, HALF], U8, name="top_bytes%d" % t, align_bytes=64, offset=base + 1024)
+            top_words.append(tw)
+            top_bytes.append(tb)
+
+        gather(top_bytes[0][:], scales[:], 0, HALF, V)
+        gather(top_words[0][:], words[:], 0, HALF + QUARTER, V)
+        quantise_w(0)
+        gather(top_bytes[1][:], scales[:], 1, HALF, V)
+        gather(top_words[1][:], words[:], 1, HALF + QUARTER, V)
+        quantise_w(1)
+        for t in (2, 3):
+            gather(top_bytes[t][:], scales[:], t, HALF, V)
+        for t in (2, 3):
+            gather(top_words[t][:], words[:], t, HALF + QUARTER, V)
+
+        groups = [
+            (0, HALF, low_words, lambda t: low_bytes[t][:]),
+            (HALF, QUARTER, mid_words, lambda t: top_bytes[t][:, 0:QUARTER]),
+            (HALF + QUARTER, QUARTER, top_words, lambda t: top_bytes[t][:, QUARTER:HALF]),
+        ]
+        accs = [psum.tile([N, width], F32, name="acc%d" % g) for g, (lo, width, ws, bs) in enumerate(groups)]
+        for t in range(D):
+            cols = slice(t * N, (t + 1) * N)
+            for g, (lo, width, ws, bs) in enumerate(groups):
                 nc.tensor.matmul_mx(
-                    out=acc[:],
+                    out=accs[g][:],
                     lhsT=w_words[:, cols].bitcast(FP8X4),
                     lhsT_scale=w_scales[:, cols],
-                    rhs=picked[h, t][0][:].bitcast(FP8X4),
-                    rhs_scale=picked[h, t][1][:],
+                    rhs=ws[t][:].bitcast(FP8X4),
+                    rhs_scale=bs(t),
                     start=(t == 0),
                     stop=(t == D - 1),
                 )
-            for q in range(2):
-                result = keep.tile([N, HALF // 2], F32, name="result%d_%d" % (h, q))
-                nc.scalar.activation(result[:], acc[:, q * 256 : (q + 1) * 256], GELU, bias=bias[:])
-                nc.sync.dma_start(out=out[:, h * HALF + q * 256 : h * HALF + (q + 1) * 256], in_=result[:])
+        for g, (lo, width, ws, bs) in enumerate(groups):
+            result = keep.tile([N, width], F32, name="result%d" % g)
+            nc.scalar.activation(result[:], accs[g][:], GELU, bias=bias[:])
+            nc.sync.dma_start(out=out[:, lo : lo + width], in_=result[:])

@@ -16,7 +16,8 @@ U8 = mybir.dt.uint8
 FP8X4 = mybir.dt.float8_e4m3fn_x4
 GELU = mybir.ActivationFunctionType.Gelu_apprx_tanh
 
-CHUNKS = [(512, 192), (512, 384), (512, 512), (512, 320), (512, 512), (512, 512), (512, 512), (256, 256), (256, 128)]
+CHUNKS = [(512, 192), (512, 384), (512, 512), (512, 320), (512, 512), (512, 384), (512, 384), (256, 256), (256, 256)]
+POOL_FROM = 5
 LOW = [(0, 128), (128, 256), (256, 512)]
 HALF, QUARTER = V // 2, V // 4
 
@@ -71,7 +72,11 @@ def tile_picked_deform_lin_gelu_def_e_kernel(tc, xT, w, b, offs, out):
             grouped = keep.tile([P, width, PACK], BF16, name="grouped%d" % i, align_bytes=64)
             if share > 0:
                 interleave(nc.scalar.copy, 2, grouped[:, 0:share, :], raw[:, :, 0:share])
-            if share < width:
+            if share < width and i >= POOL_FROM:
+                nc.gpsimd.tensor_copy(
+                    out=grouped[:, share:width, :], in_=raw[:, :, share:width].rearrange("p t c -> p c t")
+                )
+            elif share < width:
                 interleave(nc.vector.tensor_copy, 4, grouped[:, share:width, :], raw[:, :, share:width])
             nc.vector.quantize_mx(
                 out=words[:, start : start + width].bitcast(FP8X4),

@@ -16,10 +16,12 @@ U8 = mybir.dt.uint8
 FP8X4 = mybir.dt.float8_e4m3fn_x4
 GELU = mybir.ActivationFunctionType.Gelu_apprx_tanh
 
-CHUNKS = [(512, 192), (512, 384), (512, 512), (512, 320), (512, 512), (512, 384), (512, 384), (256, 256), (256, 256)]
-POOL_FROM = 5
-LOW = [(0, 128), (128, 256), (256, 512)]
-HALF, QUARTER = V // 2, V // 4
+WIDTH = 512
+LOADS = T // WIDTH
+HALF, QUARTER, EIGHTH = V // 2, V // 4, V // 8
+VECTOR_SHARE = {0: 320, 3: 192}
+POOL_SHARE = {1: 128, 5: 128, 7: 128}
+RAW_BYTES = PACK * WIDTH * 4
 
 
 def tile_picked_deform_lin_gelu_def_e_kernel(tc, xT, w, b, offs, out):
@@ -38,18 +40,17 @@ def tile_picked_deform_lin_gelu_def_e_kernel(tc, xT, w, b, offs, out):
 
         raws = []
         x_view = xT.rearrange("(p j) t -> p j t", j=PACK)
-        start = 0
-        for i, (width, share) in enumerate(CHUNKS):
-            raw = keep.tile([P, PACK, width], F32, name="raw%d" % i)
-            nc.sync.dma_start(out=raw[:], in_=x_view[:, :, start : start + width])
-            raws.append((start, raw))
-            start += width
+        for i in range(LOADS):
+            raw = late.tile([P, PACK, WIDTH], F32, name="raw%d" % i, align_bytes=64, offset=i * RAW_BYTES)
+            nc.sync.dma_start(out=raw[:], in_=x_view[:, :, i * WIDTH : (i + 1) * WIDTH])
+            raws.append(raw)
             if i == 0:
                 nc.sync.dma_start(lists[:], offs)
         w_raw = []
         half_bytes = 2 * PACK * N * 4
+        w_base = LOADS * RAW_BYTES
         for h in range(2):
-            wr = late.tile([P, 2, PACK, N], F32, name="w_raw%d" % h, align_bytes=64, offset=h * half_bytes)
+            wr = late.tile([P, 2, PACK, N], F32, name="w_raw%d" % h, align_bytes=64, offset=w_base + h * half_bytes)
             nc.sync.dma_start(out=wr[:], in_=w[2 * h : 2 * h + 2].rearrange("d (p j) m -> p d j m", j=PACK))
             w_raw.append(wr)
         nc.sync.dma_start(out=bias[:], in_=b)
@@ -64,34 +65,73 @@ def tile_picked_deform_lin_gelu_def_e_kernel(tc, xT, w, b, offs, out):
             nc.vector.tensor_copy(dst, window.indirect(lists[:, (t * V + lo) // 16 : (t * V + hi) // 16]))
 
         low_words = [keep.tile([P, HALF], U32, name="low_words%d" % t, align_bytes=64) for t in range(D)]
-        low_bytes = [keep.tile([P, HALF], U8, name="low_bytes%d" % t, align_bytes=64) for t in range(D)]
         mid_words = [keep.tile([P, QUARTER], U32, name="mid_words%d" % t, align_bytes=64) for t in range(D)]
+        low_bytes = {}
 
-        for i, (width, share) in enumerate(CHUNKS):
-            start, raw = raws[i]
-            grouped = keep.tile([P, width, PACK], BF16, name="grouped%d" % i, align_bytes=64)
-            if share > 0:
-                interleave(nc.scalar.copy, 2, grouped[:, 0:share, :], raw[:, :, 0:share])
-            if share < width and i >= POOL_FROM:
-                nc.gpsimd.tensor_copy(
-                    out=grouped[:, share:width, :], in_=raw[:, :, share:width].rearrange("p t c -> p c t")
-                )
-            elif share < width:
-                interleave(nc.vector.tensor_copy, 4, grouped[:, share:width, :], raw[:, :, share:width])
+        def bytes_tile(t, quarter, over=None):
+            name = "low_bytes%d_%d" % (t, quarter)
+            if over is None:
+                tile = keep.tile([P, QUARTER], U8, name=name, align_bytes=64)
+            else:
+                tile = late.tile([P, QUARTER], U8, name=name, align_bytes=64, offset=over * RAW_BYTES)
+            low_bytes[t, quarter] = tile[:]
+            return tile
+
+        def round_load(i):
+            grouped = keep.tile([P, WIDTH, PACK], BF16, name="grouped%d" % i, align_bytes=64)
+            own = WIDTH - VECTOR_SHARE.get(i, 0) - POOL_SHARE.get(i, 0)
+            interleave(nc.scalar.copy, 2, grouped[:, 0:own, :], raws[i][:, :, 0:own])
+            if i in VECTOR_SHARE:
+                interleave(nc.vector.tensor_copy, 4, grouped[:, own:, :], raws[i][:, :, own:])
+            if i in POOL_SHARE:
+                nc.gpsimd.tensor_copy(out=grouped[:, own:, :], in_=raws[i][:, :, own:].rearrange("p t c -> p c t"))
+            return grouped
+
+        def quantise(i, grouped):
+            cols = slice(i * WIDTH, (i + 1) * WIDTH)
             nc.vector.quantize_mx(
-                out=words[:, start : start + width].bitcast(FP8X4),
-                scales=scales[:, start : start + width],
-                in_=grouped[:].rearrange("p c t -> p (c t)"),
+                out=words[:, cols].bitcast(FP8X4), scales=scales[:, cols], in_=grouped[:].rearrange("p c t -> p (c t)")
             )
-            done = start + width
-            for lo, hi in LOW:
-                if PACK * hi == done:
-                    for t in range(D):
-                        gather(low_words[t][:, lo:hi], words[:, 0:done], t, lo, hi)
-                        gather(low_bytes[t][:, lo:hi], scales[:, 0:done], t, lo, hi)
-            if done == PACK * (HALF + QUARTER):
-                for t in range(D):
-                    gather(mid_words[t][:], words[:], t, HALF, HALF + QUARTER)
+
+        def gather_words(lo, hi):
+            for t in range(D):
+                gather(low_words[t][:, lo:hi], words[:, 0 : PACK * hi], t, lo, hi)
+
+        def gather_bytes(tile, t, lo, hi):
+            first = lo % QUARTER
+            gather(tile[:, first : first + hi - lo], scales[:, 0 : PACK * hi], t, lo, hi)
+
+        bytes0 = keep.tile([P, HALF], U8, name="low_bytes0", align_bytes=64)
+        quantise(0, round_load(0))
+        gather_words(0, EIGHTH)
+        first1 = bytes_tile(1, 0)
+        gather_bytes(bytes0, 0, 0, EIGHTH)
+        gather_bytes(first1, 1, 0, EIGHTH)
+
+        quantise(1, round_load(1))
+        first3 = bytes_tile(3, 0, over=1)
+        gather_bytes(first3, 3, 0, EIGHTH)
+        gather_words(EIGHTH, QUARTER)
+        for tile, t in ((bytes0, 0), (first1, 1), (first3, 3)):
+            gather_bytes(tile, t, EIGHTH, QUARTER)
+
+        quantise(2, round_load(2))
+        quantise(3, round_load(3))
+        gather_bytes(bytes_tile(2, 0, over=3), 2, 0, QUARTER)
+        gather_words(QUARTER, HALF)
+        gather(bytes0[:, QUARTER:HALF], scales[:, 0 : PACK * HALF], 0, QUARTER, HALF)
+
+        quantise(4, round_load(4))
+        quantise(5, round_load(5))
+        gather_bytes(bytes_tile(1, 1, over=5), 1, QUARTER, HALF)
+        for t in range(D):
+            gather(mid_words[t][:], words[:], t, HALF, HALF + QUARTER)
+
+        grouped = round_load(6)
+        gather_bytes(bytes_tile(2, 1, over=6), 2, QUARTER, HALF)
+        quantise(6, grouped)
+        quantise(7, round_load(7))
+        gather_bytes(bytes_tile(3, 1, over=7), 3, QUARTER, HALF)
 
         w_words = keep.tile([P, D * N], U32, name="w_words", align_bytes=64)
         w_scales = keep.tile([P, D * N], U8, name="w_scales", align_bytes=64)
@@ -113,7 +153,7 @@ def tile_picked_deform_lin_gelu_def_e_kernel(tc, xT, w, b, offs, out):
                 tw = keep.tile([P, QUARTER], U32, name="top_words0", align_bytes=64)
                 tb = keep.tile([P, HALF], U8, name="top_bytes0", align_bytes=64)
             else:
-                base = (t // 2) * half_bytes + (t % 2) * 2048
+                base = w_base + (t // 2) * half_bytes + (t % 2) * 2048
                 tw = late.tile([P, QUARTER], U32, name="top_words%d" % t, align_bytes=64, offset=base)
                 tb = late.tile([P, HALF], U8, name="top_bytes%d" % t, align_bytes=64, offset=base + 1024)
             top_words.append(tw)
@@ -130,25 +170,35 @@ def tile_picked_deform_lin_gelu_def_e_kernel(tc, xT, w, b, offs, out):
         for t in (2, 3):
             gather(top_words[t][:], words[:], t, HALF + QUARTER, V)
 
-        groups = [
-            (0, HALF, low_words, lambda t: low_bytes[t][:]),
-            (HALF, QUARTER, mid_words, lambda t: top_bytes[t][:, 0:QUARTER]),
-            (HALF + QUARTER, QUARTER, top_words, lambda t: top_bytes[t][:, QUARTER:HALF]),
-        ]
-        accs = [psum.tile([N, width], F32, name="acc%d" % g) for g, (lo, width, ws, bs) in enumerate(groups)]
-        for t in range(D):
+        spans = [(0, HALF), (HALF, QUARTER), (HALF + QUARTER, QUARTER)]
+        accs = [psum.tile([N, width], F32, name="acc%d" % g) for g, (lo, width) in enumerate(spans)]
+
+        def multiply(t, acc, rhs, rhs_scale, start, stop):
             cols = slice(t * N, (t + 1) * N)
-            for g, (lo, width, ws, bs) in enumerate(groups):
-                nc.tensor.matmul_mx(
-                    out=accs[g][:],
-                    lhsT=w_words[:, cols].bitcast(FP8X4),
-                    lhsT_scale=w_scales[:, cols],
-                    rhs=ws[t][:].bitcast(FP8X4),
-                    rhs_scale=bs(t),
-                    start=(t == 0),
-                    stop=(t == D - 1),
-                )
-        for g, (lo, width, ws, bs) in enumerate(groups):
+            nc.tensor.matmul_mx(
+                out=acc,
+                lhsT=w_words[:, cols].bitcast(FP8X4),
+                lhsT_scale=w_scales[:, cols],
+                rhs=rhs.bitcast(FP8X4),
+                rhs_scale=rhs_scale,
+                start=start,
+                stop=stop,
+            )
+
+        for pair in ((0, 1), (2, 3)):
+            for t in pair:
+                if t == 0:
+                    multiply(t, accs[0][:], low_words[t][:], bytes0[:], True, False)
+                else:
+                    for quarter in range(2):
+                        cols = slice(quarter * QUARTER, (quarter + 1) * QUARTER)
+                        last = t == D - 1 and quarter == 1
+                        multiply(t, accs[0][:, cols], low_words[t][:, cols], low_bytes[t, quarter], False, last)
+            for t in pair:
+                multiply(t, accs[1][:], mid_words[t][:], top_bytes[t][:, 0:QUARTER], t == 0, t == D - 1)
+            for t in pair:
+                multiply(t, accs[2][:], top_words[t][:], top_bytes[t][:, QUARTER:HALF], t == 0, t == D - 1)
+        for g, (lo, width) in enumerate(spans):
             result = keep.tile([N, width], F32, name="result%d" % g)
             nc.scalar.activation(result[:], accs[g][:], GELU, bias=bias[:])
             nc.sync.dma_start(out=out[:, lo : lo + width], in_=result[:])

@@ -16,12 +16,10 @@ U8 = mybir.dt.uint8
 FP8X4 = mybir.dt.float8_e4m3fn_x4
 GELU = mybir.ActivationFunctionType.Gelu_apprx_tanh
 
-WIDTH = 512
-LOADS = T // WIDTH
+WIDTHS = [512] * 7 + [256] * 2
 HALF, QUARTER, EIGHTH = V // 2, V // 4, V // 8
-VECTOR_SHARE = {0: 320, 3: 192}
-POOL_SHARE = {1: 128, 5: 128, 7: 128}
-RAW_BYTES = PACK * WIDTH * 4
+VECTOR_SHARE = {0: 256, 3: 128, 5: 64}
+POOL_LOAD, POOL_SHARE = 6, 128
 
 
 def tile_picked_deform_lin_gelu_def_e_kernel(tc, xT, w, b, offs, out):
@@ -38,17 +36,22 @@ def tile_picked_deform_lin_gelu_def_e_kernel(tc, xT, w, b, offs, out):
 
         nc.gpsimd.memset(scales[:].bitcast(I32), 0)
 
-        raws = []
+        raws, starts = [], []
         x_view = xT.rearrange("(p j) t -> p j t", j=PACK)
-        for i in range(LOADS):
-            raw = late.tile([P, PACK, WIDTH], F32, name="raw%d" % i, align_bytes=64, offset=i * RAW_BYTES)
-            nc.sync.dma_start(out=raw[:], in_=x_view[:, :, i * WIDTH : (i + 1) * WIDTH])
+        for i, width in enumerate(WIDTHS):
+            start = sum(WIDTHS[:i])
+            if i == POOL_LOAD:
+                raw = late.tile([P, PACK, width], F32, name="raw%d" % i, align_bytes=64, offset=0)
+            else:
+                raw = keep.tile([P, PACK, width], F32, name="raw%d" % i)
+            nc.sync.dma_start(out=raw[:], in_=x_view[:, :, start : start + width])
             raws.append(raw)
+            starts.append(start)
             if i == 0:
                 nc.sync.dma_start(lists[:], offs)
         w_raw = []
         half_bytes = 2 * PACK * N * 4
-        w_base = LOADS * RAW_BYTES
+        w_base = PACK * WIDTHS[POOL_LOAD] * 4
         for h in range(2):
             wr = late.tile([P, 2, PACK, N], F32, name="w_raw%d" % h, align_bytes=64, offset=w_base + h * half_bytes)
             nc.sync.dma_start(out=wr[:], in_=w[2 * h : 2 * h + 2].rearrange("d (p j) m -> p d j m", j=PACK))
@@ -66,72 +69,59 @@ def tile_picked_deform_lin_gelu_def_e_kernel(tc, xT, w, b, offs, out):
 
         low_words = [keep.tile([P, HALF], U32, name="low_words%d" % t, align_bytes=64) for t in range(D)]
         mid_words = [keep.tile([P, QUARTER], U32, name="mid_words%d" % t, align_bytes=64) for t in range(D)]
-        low_bytes = {}
+        low_bytes = [keep.tile([P, HALF], U8, name="low_bytes%d" % t, align_bytes=64) for t in range(D)]
 
-        def bytes_tile(t, quarter, over=None):
-            name = "low_bytes%d_%d" % (t, quarter)
-            if over is None:
-                tile = keep.tile([P, QUARTER], U8, name=name, align_bytes=64)
-            else:
-                tile = late.tile([P, QUARTER], U8, name=name, align_bytes=64, offset=over * RAW_BYTES)
-            low_bytes[t, quarter] = tile[:]
-            return tile
+        wide = WIDTHS[POOL_LOAD]
+        shared = keep.tile([P, 2 * wide - POOL_SHARE, PACK], BF16, name="shared", align_bytes=64)
 
         def round_load(i):
-            grouped = keep.tile([P, WIDTH, PACK], BF16, name="grouped%d" % i, align_bytes=64)
-            own = WIDTH - VECTOR_SHARE.get(i, 0) - POOL_SHARE.get(i, 0)
-            interleave(nc.scalar.copy, 2, grouped[:, 0:own, :], raws[i][:, :, 0:own])
-            if i in VECTOR_SHARE:
-                interleave(nc.vector.tensor_copy, 4, grouped[:, own:, :], raws[i][:, :, own:])
-            if i in POOL_SHARE:
-                nc.gpsimd.tensor_copy(out=grouped[:, own:, :], in_=raws[i][:, :, own:].rearrange("p t c -> p c t"))
+            width, raw = WIDTHS[i], raws[i]
+            if i == POOL_LOAD:
+                grouped = shared[:, wide - POOL_SHARE :, :]
+                nc.gpsimd.tensor_copy(
+                    out=grouped[:, 0:POOL_SHARE, :], in_=raw[:, :, 0:POOL_SHARE].rearrange("p t c -> p c t")
+                )
+                interleave(nc.scalar.copy, 2, grouped[:, POOL_SHARE:, :], raw[:, :, POOL_SHARE:])
+                return grouped
+            if i == POOL_LOAD - 1:
+                grouped = shared[:, 0:wide, :]
+            else:
+                grouped = keep.tile([P, width, PACK], BF16, name="grouped%d" % i, align_bytes=64)[:]
+            own = width - VECTOR_SHARE.get(i, 0)
+            interleave(nc.scalar.copy, 2, grouped[:, 0:own, :], raw[:, :, 0:own])
+            if own < width:
+                interleave(nc.vector.tensor_copy, 4, grouped[:, own:, :], raw[:, :, own:])
             return grouped
 
         def quantise(i, grouped):
-            cols = slice(i * WIDTH, (i + 1) * WIDTH)
+            cols = slice(starts[i], starts[i] + WIDTHS[i])
             nc.vector.quantize_mx(
-                out=words[:, cols].bitcast(FP8X4), scales=scales[:, cols], in_=grouped[:].rearrange("p c t -> p (c t)")
+                out=words[:, cols].bitcast(FP8X4), scales=scales[:, cols], in_=grouped.rearrange("p c t -> p (c t)")
             )
 
-        def gather_words(lo, hi):
+        def gather_low(lo, hi, byte_taps):
             for t in range(D):
                 gather(low_words[t][:, lo:hi], words[:, 0 : PACK * hi], t, lo, hi)
+            for t in byte_taps:
+                gather(low_bytes[t][:, lo:hi], scales[:, 0 : PACK * hi], t, lo, hi)
 
-        def gather_bytes(tile, t, lo, hi):
-            first = lo % QUARTER
-            gather(tile[:, first : first + hi - lo], scales[:, 0 : PACK * hi], t, lo, hi)
-
-        bytes0 = keep.tile([P, HALF], U8, name="low_bytes0", align_bytes=64)
         quantise(0, round_load(0))
-        gather_words(0, EIGHTH)
-        first1 = bytes_tile(1, 0)
-        gather_bytes(bytes0, 0, 0, EIGHTH)
-        gather_bytes(first1, 1, 0, EIGHTH)
-
+        gather_low(0, EIGHTH, range(D))
         quantise(1, round_load(1))
-        first3 = bytes_tile(3, 0, over=1)
-        gather_bytes(first3, 3, 0, EIGHTH)
-        gather_words(EIGHTH, QUARTER)
-        for tile, t in ((bytes0, 0), (first1, 1), (first3, 3)):
-            gather_bytes(tile, t, EIGHTH, QUARTER)
-
+        gather_low(EIGHTH, QUARTER, range(D))
         quantise(2, round_load(2))
         quantise(3, round_load(3))
-        gather_bytes(bytes_tile(2, 0, over=3), 2, 0, QUARTER)
-        gather_words(QUARTER, HALF)
-        gather(bytes0[:, QUARTER:HALF], scales[:, 0 : PACK * HALF], 0, QUARTER, HALF)
-
+        gather_low(QUARTER, HALF, range(D - 1))
         quantise(4, round_load(4))
         quantise(5, round_load(5))
-        gather_bytes(bytes_tile(1, 1, over=5), 1, QUARTER, HALF)
         for t in range(D):
             gather(mid_words[t][:], words[:], t, HALF, HALF + QUARTER)
-
         grouped = round_load(6)
-        gather_bytes(bytes_tile(2, 1, over=6), 2, QUARTER, HALF)
+        held_bytes = late.tile([P, QUARTER], U8, name="held_bytes", align_bytes=64, offset=0)
+        gather(held_bytes[:], scales[:, 0 : PACK * HALF], D - 1, QUARTER, HALF)
         quantise(6, grouped)
         quantise(7, round_load(7))
-        gather_bytes(bytes_tile(3, 1, over=7), 3, QUARTER, HALF)
+        quantise(8, round_load(8))
 
         w_words = keep.tile([P, D * N], U32, name="w_words", align_bytes=64)
         w_scales = keep.tile([P, D * N], U8, name="w_scales", align_bytes=64)
@@ -187,13 +177,11 @@ def tile_picked_deform_lin_gelu_def_e_kernel(tc, xT, w, b, offs, out):
 
         for pair in ((0, 1), (2, 3)):
             for t in pair:
-                if t == 0:
-                    multiply(t, accs[0][:], low_words[t][:], bytes0[:], True, False)
+                if t < D - 1:
+                    multiply(t, accs[0][:], low_words[t][:], low_bytes[t][:], t == 0, False)
                 else:
-                    for quarter in range(2):
-                        cols = slice(quarter * QUARTER, (quarter + 1) * QUARTER)
-                        last = t == D - 1 and quarter == 1
-                        multiply(t, accs[0][:, cols], low_words[t][:, cols], low_bytes[t, quarter], False, last)
+                    multiply(t, accs[0][:, 0:QUARTER], low_words[t][:, 0:QUARTER], low_bytes[t][:, 0:QUARTER], False, False)
+                    multiply(t, accs[0][:, QUARTER:], low_words[t][:, QUARTER:], held_bytes[:], False, True)
             for t in pair:
                 multiply(t, accs[1][:], mid_words[t][:], top_bytes[t][:, 0:QUARTER], t == 0, t == D - 1)
             for t in pair:

@@ -145,7 +145,8 @@ def tile_picked_deform_lin_gelu_def_e_kernel(tc, xT, w, b, offs, out):
             else:
                 base = w_base + (t // 2) * half_bytes + (t % 2) * 2048
                 tw = late.tile([P, QUARTER], U32, name="top_words%d" % t, align_bytes=64, offset=base)
-                tb = late.tile([P, HALF], U8, name="top_bytes%d" % t, align_bytes=64, offset=base + 1024)
+                place = w_base if t == 2 else base + 1024
+                tb = late.tile([P, HALF], U8, name="top_bytes%d" % t, align_bytes=64, offset=place)
             top_words.append(tw)
             top_bytes.append(tb)
 
@@ -154,9 +155,9 @@ def tile_picked_deform_lin_gelu_def_e_kernel(tc, xT, w, b, offs, out):
         quantise_w(0)
         gather(top_bytes[1][:], scales[:], 1, HALF, V)
         gather(top_words[1][:], words[:], 1, HALF + QUARTER, V)
+        gather(top_bytes[2][:], scales[:], 2, HALF, V)
         quantise_w(1)
-        for t in (2, 3):
-            gather(top_bytes[t][:], scales[:], t, HALF, V)
+        gather(top_bytes[3][:], scales[:], 3, HALF, V)
         for t in (2, 3):
             gather(top_words[t][:], words[:], t, HALF + QUARTER, V)
 

@@ -18,44 +18,40 @@ GELU = mybir.ActivationFunctionType.Gelu_apprx_tanh
 
 WIDTHS = [512] * 7 + [256] * 2
 HALF, QUARTER, EIGHTH = V // 2, V // 4, V // 8
-VECTOR_SHARE = {0: 256, 3: 128, 5: 64}
-POOL_LOAD, POOL_SHARE = 6, 128
+FIRST_VECTOR_SHARE = 320
+POOL_SHARE = [0, 192, 192, 192, 128, 224, 224, 0, 96]
 
 
 def tile_picked_deform_lin_gelu_def_e_kernel(tc, xT, w, b, offs, out):
     nc = tc.nc
     with ExitStack() as ctx:
         keep = ctx.enter_context(tc.tile_pool(name="keep", bufs=1))
-        late = ctx.enter_context(tc.tile_pool(name="late", bufs=1))
+        loads = ctx.enter_context(tc.tile_pool(name="loads", bufs=1))
         psum = ctx.enter_context(tc.psum_pool(name="psum", bufs=1))
 
         lists = keep.tile([P, D * V // 16], U16, name="lists")
         words = keep.tile([P, T], U32, name="words", align_bytes=64)
         scales = keep.tile([P, T], U8, name="scales", align_bytes=64)
         bias = keep.tile([P, 1], F32, name="bias")
-
         nc.gpsimd.memset(scales[:].bitcast(I32), 0)
 
-        raws, starts = [], []
+        starts = [sum(WIDTHS[:i]) for i in range(len(WIDTHS))]
+        column_bytes = PACK * 4
         x_view = xT.rearrange("(p j) t -> p j t", j=PACK)
+        raws = []
         for i, width in enumerate(WIDTHS):
-            start = sum(WIDTHS[:i])
-            if i == POOL_LOAD:
-                raw = late.tile([P, PACK, width], F32, name="raw%d" % i, align_bytes=64, offset=0)
-            else:
-                raw = keep.tile([P, PACK, width], F32, name="raw%d" % i)
-            nc.sync.dma_start(out=raw[:], in_=x_view[:, :, start : start + width])
+            raw = loads.tile([P, PACK, width], F32, name="raw%d" % i, align_bytes=64, offset=starts[i] * column_bytes)
+            nc.sync.dma_start(out=raw[:], in_=x_view[:, :, starts[i] : starts[i] + width])
             raws.append(raw)
-            starts.append(start)
             if i == 0:
                 nc.sync.dma_start(lists[:], offs)
-        w_raw = []
-        half_bytes = 2 * PACK * N * 4
-        w_base = PACK * WIDTHS[POOL_LOAD] * 4
+        w_raw, w_place = [], []
         for h in range(2):
-            wr = late.tile([P, 2, PACK, N], F32, name="w_raw%d" % h, align_bytes=64, offset=w_base + h * half_bytes)
+            place = (T + 2 * N * h) * column_bytes
+            wr = loads.tile([P, 2, PACK, N], F32, name="w_raw%d" % h, align_bytes=64, offset=place)
             nc.sync.dma_start(out=wr[:], in_=w[2 * h : 2 * h + 2].rearrange("d (p j) m -> p d j m", j=PACK))
             w_raw.append(wr)
+            w_place.append(place)
         nc.sync.dma_start(out=bias[:], in_=b)
 
         def interleave(copy, run, dst, src):
@@ -64,64 +60,86 @@ def tile_picked_deform_lin_gelu_def_e_kernel(tc, xT, w, b, offs, out):
                 in_=src.rearrange("p t (c i) -> p c t i", i=run),
             )
 
-        def gather(dst, window, t, lo, hi):
-            nc.vector.tensor_copy(dst, window.indirect(lists[:, (t * V + lo) // 16 : (t * V + hi) // 16]))
+        bases = [starts[i] - sum(POOL_SHARE[: i + 1]) for i in range(len(WIDTHS))]
+        staged = keep.tile([P, T - sum(POOL_SHARE), PACK], BF16, name="staged", align_bytes=64)
 
-        low_words = [keep.tile([P, HALF], U32, name="low_words%d" % t, align_bytes=64) for t in range(D)]
-        mid_words = [keep.tile([P, QUARTER], U32, name="mid_words%d" % t, align_bytes=64) for t in range(D)]
-        low_bytes = [keep.tile([P, HALF], U8, name="low_bytes%d" % t, align_bytes=64) for t in range(D)]
-
-        wide = WIDTHS[POOL_LOAD]
-        shared = keep.tile([P, 2 * wide - POOL_SHARE, PACK], BF16, name="shared", align_bytes=64)
-
-        def round_load(i):
-            width, raw = WIDTHS[i], raws[i]
-            if i == POOL_LOAD:
-                grouped = shared[:, wide - POOL_SHARE :, :]
-                nc.gpsimd.tensor_copy(
-                    out=grouped[:, 0:POOL_SHARE, :], in_=raw[:, :, 0:POOL_SHARE].rearrange("p t c -> p c t")
-                )
-                interleave(nc.scalar.copy, 2, grouped[:, POOL_SHARE:, :], raw[:, :, POOL_SHARE:])
-                return grouped
-            if i == POOL_LOAD - 1:
-                grouped = shared[:, 0:wide, :]
-            else:
-                grouped = keep.tile([P, width, PACK], BF16, name="grouped%d" % i, align_bytes=64)[:]
-            own = width - VECTOR_SHARE.get(i, 0)
-            interleave(nc.scalar.copy, 2, grouped[:, 0:own, :], raw[:, :, 0:own])
+        def quantise(i):
+            width, raw, pool = WIDTHS[i], raws[i], POOL_SHARE[i]
+            grouped = staged[:, bases[i] : bases[i] + width, :]
+            own = width - (FIRST_VECTOR_SHARE if i == 0 else 0)
+            if pool:
+                nc.gpsimd.tensor_copy(out=grouped[:, 0:pool, :], in_=raw[:, :, 0:pool].rearrange("p t c -> p c t"))
+            interleave(nc.scalar.copy, 2, grouped[:, pool:own, :], raw[:, :, pool:own])
             if own < width:
                 interleave(nc.vector.tensor_copy, 4, grouped[:, own:, :], raw[:, :, own:])
-            return grouped
-
-        def quantise(i, grouped):
-            cols = slice(starts[i], starts[i] + WIDTHS[i])
+            cols = slice(starts[i], starts[i] + width)
             nc.vector.quantize_mx(
                 out=words[:, cols].bitcast(FP8X4), scales=scales[:, cols], in_=grouped.rearrange("p c t -> p (c t)")
             )
 
-        def gather_low(lo, hi, byte_taps):
-            for t in range(D):
-                gather(low_words[t][:, lo:hi], words[:, 0 : PACK * hi], t, lo, hi)
-            for t in byte_taps:
-                gather(low_bytes[t][:, lo:hi], scales[:, 0 : PACK * hi], t, lo, hi)
+        pieces = {(sort, t): [] for sort in "wb" for t in range(D)}
 
-        quantise(0, round_load(0))
-        gather_low(0, EIGHTH, range(D))
-        quantise(1, round_load(1))
-        gather_low(EIGHTH, QUARTER, range(D))
-        quantise(2, round_load(2))
-        quantise(3, round_load(3))
-        gather_low(QUARTER, HALF, range(D - 1))
-        quantise(4, round_load(4))
-        quantise(5, round_load(5))
+        def room(sort, t, lo, hi, place=None):
+            dtype = U32 if sort == "w" else U8
+            name = "%s%d_%d" % (sort, t, lo)
+            if place is None:
+                tile = keep.tile([P, hi - lo], dtype, name=name, align_bytes=64)
+            else:
+                tile = loads.tile([P, hi - lo], dtype, name=name, align_bytes=64, offset=place)
+            pieces[(sort, t)].append((lo, hi, tile))
+            return tile
+
+        def part(sort, t, lo, hi):
+            for a, z, tile in pieces[(sort, t)]:
+                if a <= lo and hi <= z:
+                    return tile[:, lo - a : hi - a]
+            raise ValueError("no tile holds this range")
+
+        def gather(sort, t, lo, hi, whole=False):
+            table = words if sort == "w" else scales
+            window = table[:] if whole else table[:, 0 : PACK * hi]
+            nc.vector.tensor_copy(part(sort, t, lo, hi), window.indirect(lists[:, (t * V + lo) // 16 : (t * V + hi) // 16]))
+
+        cut = HALF - EIGHTH
+        for t in (0, 1):
+            room("w", t, 0, HALF)
+            room("w", t, HALF, HALF + QUARTER)
+            room("b", t, 0, HALF)
+            room("b", t, HALF, V)
+        room("w", 2, 0, HALF + QUARTER)
+        room("w", 3, 0, cut)
+        for t in (2, 3):
+            room("b", t, 0, QUARTER)
+
+        quantise(0)
+        for sort in "wb":
+            for t in range(D):
+                gather(sort, t, 0, EIGHTH)
+        quantise(1)
+        for t in (0, 1):
+            gather("w", t, EIGHTH, QUARTER)
         for t in range(D):
-            gather(mid_words[t][:], words[:], t, HALF, HALF + QUARTER)
-        grouped = round_load(6)
-        held_bytes = late.tile([P, QUARTER], U8, name="held_bytes", align_bytes=64, offset=0)
-        gather(held_bytes[:], scales[:, 0 : PACK * HALF], D - 1, QUARTER, HALF)
-        quantise(6, grouped)
-        quantise(7, round_load(7))
-        quantise(8, round_load(8))
+            gather("b", t, EIGHTH, QUARTER)
+        quantise(2)
+        for t in (2, 3):
+            gather("w", t, EIGHTH, cut)
+        quantise(3)
+        for sort in "wb":
+            for t in (0, 1):
+                gather(sort, t, QUARTER, HALF)
+        quantise(4)
+        for t in (2, 3):
+            room("b", t, QUARTER, HALF, starts[4] * column_bytes + t * QUARTER)
+            gather("b", t, QUARTER, HALF)
+        quantise(5)
+        for t in (0, 1):
+            gather("w", t, HALF, HALF + QUARTER, whole=True)
+        gather("w", 2, cut, HALF + QUARTER)
+        quantise(6)
+        quantise(7)
+        room("w", 3, cut, HALF + QUARTER, starts[7] * column_bytes)
+        gather("w", 3, cut, HALF + QUARTER)
+        quantise(8)
 
         w_words = keep.tile([P, D * N], U32, name="w_words", align_bytes=64)
         w_scales = keep.tile([P, D * N], U8, name="w_scales", align_bytes=64)
@@ -137,57 +155,52 @@ def tile_picked_deform_lin_gelu_def_e_kernel(tc, xT, w, b, offs, out):
                 in_=w_grouped[:, 2 * h : 2 * h + 2].rearrange("p d m t -> p (d m t)"),
             )
 
-        top_words, top_bytes = [], []
-        for t in range(D):
-            if t == 0:
-                tw = keep.tile([P, QUARTER], U32, name="top_words0", align_bytes=64)
-                tb = keep.tile([P, HALF], U8, name="top_bytes0", align_bytes=64)
-            else:
-                base = w_base + (t // 2) * half_bytes + (t % 2) * 2048
-                tw = late.tile([P, QUARTER], U32, name="top_words%d" % t, align_bytes=64, offset=base)
-                place = w_base if t == 2 else base + 1024
-                tb = late.tile([P, HALF], U8, name="top_bytes%d" % t, align_bytes=64, offset=place)
-            top_words.append(tw)
-            top_bytes.append(tb)
-
-        gather(top_bytes[0][:], scales[:], 0, HALF, V)
-        gather(top_words[0][:], words[:], 0, HALF + QUARTER, V)
+        for t in (0, 1):
+            gather("b", t, HALF, V)
         quantise_w(0)
-        gather(top_bytes[1][:], scales[:], 1, HALF, V)
-        gather(top_words[1][:], words[:], 1, HALF + QUARTER, V)
-        gather(top_bytes[2][:], scales[:], 2, HALF, V)
-        quantise_w(1)
-        gather(top_bytes[3][:], scales[:], 3, HALF, V)
         for t in (2, 3):
-            gather(top_words[t][:], words[:], t, HALF + QUARTER, V)
+            room("b", t, HALF, V, w_place[0] + (t % 2) * HALF)
+            gather("b", t, HALF, V)
+        quantise_w(1)
+        for t in range(D):
+            room("w", t, HALF + QUARTER, V, w_place[1] + t * QUARTER * 4)
+            gather("w", t, HALF + QUARTER, V)
 
-        spans = [(0, HALF), (HALF, QUARTER), (HALF + QUARTER, QUARTER)]
-        accs = [psum.tile([N, width], F32, name="acc%d" % g) for g, (lo, width) in enumerate(spans)]
+        spans = [(0, HALF), (HALF, HALF + QUARTER), (HALF + QUARTER, V)]
+        accs = [psum.tile([N, hi - lo], F32, name="acc%d" % g) for g, (lo, hi) in enumerate(spans)]
 
-        def multiply(t, acc, rhs, rhs_scale, start, stop):
+        def multiply(g, t):
+            lo, hi = spans[g]
+            edges = sorted({e for sort in "wb" for a, z, tile in pieces[(sort, t)] for e in (a, z) if lo <= e <= hi} | {lo, hi})
+            runs = []
+            for a, z in zip(edges, edges[1:]):
+                if z - a == cut:
+                    runs.extend([(a, a + QUARTER), (a + QUARTER, z)])
+                else:
+                    runs.append((a, z))
             cols = slice(t * N, (t + 1) * N)
-            nc.tensor.matmul_mx(
-                out=acc,
-                lhsT=w_words[:, cols].bitcast(FP8X4),
-                lhsT_scale=w_scales[:, cols],
-                rhs=rhs.bitcast(FP8X4),
-                rhs_scale=rhs_scale,
-                start=start,
-                stop=stop,
-            )
+            for a, z in runs:
+                nc.tensor.matmul_mx(
+                    out=accs[g][:, a - lo : z - lo],
+                    lhsT=w_words[:, cols].bitcast(FP8X4),
+                    lhsT_scale=w_scales[:, cols],
+                    rhs=part("w", t, a, z).bitcast(FP8X4),
+                    rhs_scale=part("b", t, a, z),
+                    start=(t == 0 and a == lo),
+                    stop=(t == D - 1 and z == hi),
+                )
+
+        def finish(g):
+            lo, hi = spans[g]
+            result = keep.tile([N, hi - lo], F32, name="result%d" % g)
+            nc.scalar.activation(result[:], accs[g][:], GELU, bias=bias[:])
+            nc.sync.dma_start(out=out[:, lo:hi], in_=result[:])
 
         for pair in ((0, 1), (2, 3)):
-            for t in pair:
-                if t < D - 1:
-                    multiply(t, accs[0][:], low_words[t][:], low_bytes[t][:], t == 0, False)
-                else:
-                    multiply(t, accs[0][:, 0:QUARTER], low_words[t][:, 0:QUARTER], low_bytes[t][:, 0:QUARTER], False, False)
-                    multiply(t, accs[0][:, QUARTER:], low_words[t][:, QUARTER:], held_bytes[:], False, True)
-            for t in pair:
-                multiply(t, accs[1][:], mid_words[t][:], top_bytes[t][:, 0:QUARTER], t == 0, t == D - 1)
-            for t in pair:
-                multiply(t, accs[2][:], top_words[t][:], top_bytes[t][:, QUARTER:HALF], t == 0, t == D - 1)
-        for g, (lo, width) in enumerate(spans):
-            result = keep.tile([N, width], F32, name="result%d" % g)
-            nc.scalar.activation(result[:], accs[g][:], GELU, bias=bias[:])
-            nc.sync.dma_start(out=out[:, lo : lo + width], in_=result[:])
+            for g in (0, 1):
+                for t in pair:
+                    multiply(g, t)
+        for t in range(D):
+            multiply(2, t)
+        for g in range(len(spans)):
+            finish(g)

@@ -19,7 +19,7 @@ GELU = mybir.ActivationFunctionType.Gelu_apprx_tanh
 WIDTHS = [512] * 7 + [256] * 2
 HALF, QUARTER, EIGHTH = V // 2, V // 4, V // 8
 FIRST_VECTOR_SHARE = 320
-POOL_SHARE = [0, 192, 192, 192, 128, 224, 224, 0, 96]
+POOL_SHARE = [0, 192, 192, 192, 192, 208, 224, 0, 64]
 
 
 def tile_picked_deform_lin_gelu_def_e_kernel(tc, xT, w, b, offs, out):
@@ -104,7 +104,7 @@ def tile_picked_deform_lin_gelu_def_e_kernel(tc, xT, w, b, offs, out):
         for t in (0, 1):
             room("w", t, 0, HALF)
             room("w", t, HALF, HALF + QUARTER)
-            room("b", t, 0, HALF)
+            room("b", t, 0, HALF if t == 0 else QUARTER)
             room("b", t, HALF, V)
         room("w", 2, 0, HALF + QUARTER)
         room("w", 3, 0, cut)
@@ -124,11 +124,11 @@ def tile_picked_deform_lin_gelu_def_e_kernel(tc, xT, w, b, offs, out):
         for t in (2, 3):
             gather("w", t, EIGHTH, cut)
         quantise(3)
-        for sort in "wb":
-            for t in (0, 1):
-                gather(sort, t, QUARTER, HALF)
+        for t in (0, 1):
+            gather("w", t, QUARTER, HALF)
+        gather("b", 0, QUARTER, HALF)
         quantise(4)
-        for t in (2, 3):
+        for t in (1, 2, 3):
             room("b", t, QUARTER, HALF, starts[4] * column_bytes + t * QUARTER)
             gather("b", t, QUARTER, HALF)
         quantise(5)

@@ -18,8 +18,8 @@ GELU = mybir.ActivationFunctionType.Gelu_apprx_tanh
 
 WIDTHS = [512] * 7 + [256] * 2
 HALF, QUARTER, EIGHTH = V // 2, V // 4, V // 8
-FIRST_VECTOR_SHARE = 320
-POOL_SHARE = [0, 192, 192, 192, 192, 208, 224, 0, 64]
+VECTOR_SHARE = [320, 0, 0, 0, 0, 0, 0, 0, 128]
+POOL_SHARE = [0, 192, 192, 192, 192, 192, 192, 0, 0]
 
 
 def tile_picked_deform_lin_gelu_def_e_kernel(tc, xT, w, b, offs, out):
@@ -66,7 +66,7 @@ def tile_picked_deform_lin_gelu_def_e_kernel(tc, xT, w, b, offs, out):
         def quantise(i):
             width, raw, pool = WIDTHS[i], raws[i], POOL_SHARE[i]
             grouped = staged[:, bases[i] : bases[i] + width, :]
-            own = width - (FIRST_VECTOR_SHARE if i == 0 else 0)
+            own = width - VECTOR_SHARE[i]
             if pool:
                 nc.gpsimd.tensor_copy(out=grouped[:, 0:pool, :], in_=raw[:, :, 0:pool].rearrange("p t c -> p c t"))
             interleave(nc.scalar.copy, 2, grouped[:, pool:own, :], raw[:, :, pool:own])
@@ -106,9 +106,8 @@ def tile_picked_deform_lin_gelu_def_e_kernel(tc, xT, w, b, offs, out):
             room("w", t, HALF, HALF + QUARTER)
             room("b", t, 0, HALF if t == 0 else QUARTER)
             room("b", t, HALF, V)
-        room("w", 2, 0, HALF + QUARTER)
-        room("w", 3, 0, cut)
         for t in (2, 3):
+            room("w", t, 0, HALF + QUARTER)
             room("b", t, 0, QUARTER)
 
         quantise(0)
@@ -134,12 +133,10 @@ def tile_picked_deform_lin_gelu_def_e_kernel(tc, xT, w, b, offs, out):
         quantise(5)
         for t in (0, 1):
             gather("w", t, HALF, HALF + QUARTER, whole=True)
-        gather("w", 2, cut, HALF + QUARTER)
-        quantise(6)
-        quantise(7)
-        room("w", 3, cut, HALF + QUARTER, starts[7] * column_bytes)
-        gather("w", 3, cut, HALF + QUARTER)
-        quantise(8)
+        for t in (2, 3):
+            gather("w", t, cut, HALF + QUARTER)
+        for i in (6, 7, 8):
+            quantise(i)
 
         w_words = keep.tile([P, D * N], U32, name="w_words", align_bytes=64)
         w_scales = keep.tile([P, D * N], U8, name="w_scales", align_bytes=64)
@@ -172,14 +169,8 @@ def tile_picked_deform_lin_gelu_def_e_kernel(tc, xT, w, b, offs, out):
         def multiply(g, t):
             lo, hi = spans[g]
             edges = sorted({e for sort in "wb" for a, z, tile in pieces[(sort, t)] for e in (a, z) if lo <= e <= hi} | {lo, hi})
-            runs = []
-            for a, z in zip(edges, edges[1:]):
-                if z - a == cut:
-                    runs.extend([(a, a + QUARTER), (a + QUARTER, z)])
-                else:
-                    runs.append((a, z))
             cols = slice(t * N, (t + 1) * N)
-            for a, z in runs:
+            for a, z in zip(edges, edges[1:]):
                 nc.tensor.matmul_mx(
                     out=accs[g][:, a - lo : z - lo],
                     lhsT=w_words[:, cols].bitcast(FP8X4),

@@ -18,7 +18,7 @@ GELU = mybir.ActivationFunctionType.Gelu_apprx_tanh
 
 WIDTHS = [512] * 7 + [256] * 2
 HALF, QUARTER, EIGHTH = V // 2, V // 4, V // 8
-VECTOR_SHARE = [320, 0, 0, 0, 0, 0, 0, 0, 128]
+VECTOR_SHARE = [320, 0, 0, 0, 0, 0, 0, 0, 64]
 POOL_SHARE = [0, 192, 192, 192, 192, 192, 192, 0, 0]
 
 

@@ -18,7 +18,7 @@ GELU = mybir.ActivationFunctionType.Gelu_apprx_tanh
 
 WIDTHS = [512] * 7 + [256] * 2
 HALF, QUARTER, EIGHTH = V // 2, V // 4, V // 8
-VECTOR_SHARE = [320, 0, 0, 0, 0, 0, 0, 0, 64]
+VECTOR_SHARE = [320, 0, 0, 0, 0, 0, 0, 0, 48]
 POOL_SHARE = [0, 192, 192, 192, 192, 192, 192, 0, 0]
 
 
@@ -104,21 +104,26 @@ def tile_picked_deform_lin_gelu_def_e_kernel(tc, xT, w, b, offs, out):
         for t in (0, 1):
             room("w", t, 0, HALF)
             room("w", t, HALF, HALF + QUARTER)
-            room("b", t, 0, HALF if t == 0 else QUARTER)
             room("b", t, HALF, V)
         for t in (2, 3):
             room("w", t, 0, HALF + QUARTER)
-            room("b", t, 0, QUARTER)
+        room("b", 0, 0, HALF)
+        room("b", 1, 0, QUARTER)
+        for t in (2, 3):
+            room("b", t, 0, EIGHTH)
+
+        def held(t, lo, hi, i):
+            room("b", t, lo, hi, starts[i] * column_bytes + t * QUARTER)
+            gather("b", t, lo, hi)
 
         quantise(0)
         for sort in "wb":
             for t in range(D):
                 gather(sort, t, 0, EIGHTH)
         quantise(1)
-        for t in (0, 1):
-            gather("w", t, EIGHTH, QUARTER)
-        for t in range(D):
-            gather("b", t, EIGHTH, QUARTER)
+        for sort in "wb":
+            for t in (0, 1):
+                gather(sort, t, EIGHTH, QUARTER)
         quantise(2)
         for t in (2, 3):
             gather("w", t, EIGHTH, cut)
@@ -128,15 +133,16 @@ def tile_picked_deform_lin_gelu_def_e_kernel(tc, xT, w, b, offs, out):
         gather("b", 0, QUARTER, HALF)
         quantise(4)
         for t in (1, 2, 3):
-            room("b", t, QUARTER, HALF, starts[4] * column_bytes + t * QUARTER)
-            gather("b", t, QUARTER, HALF)
+            held(t, QUARTER, HALF, 4)
         quantise(5)
+        held(2, EIGHTH, QUARTER, 5)
         for t in (0, 1):
             gather("w", t, HALF, HALF + QUARTER, whole=True)
         for t in (2, 3):
             gather("w", t, cut, HALF + QUARTER)
         for i in (6, 7, 8):
             quantise(i)
+        held(3, EIGHTH, QUARTER, 8)
 
         w_words = keep.tile([P, D * N], U32, name="w_words", align_bytes=64)
         w_scales = keep.tile([P, D * N], U8, name="w_scales", align_bytes=64)

from contextlib import ExitStack

import concourse.mybir as mybir

K, T, D, V, N = 512, 4096, 4, 1024, 128
P = 128
PACK = 4
FLOPS = 2 * D * K * N * V

F32 = mybir.dt.float32
BF16 = mybir.dt.bfloat16
I32 = mybir.dt.int32
U32 = mybir.dt.uint32
U16 = mybir.dt.uint16
U8 = mybir.dt.uint8
FP8X4 = mybir.dt.float8_e4m3fn_x4
GELU = mybir.ActivationFunctionType.Gelu_apprx_tanh

WIDTHS = [512] * 7 + [256] * 2
HALF, QUARTER, EIGHTH = V // 2, V // 4, V // 8
VECTOR_SHARE = [320, 0, 0, 0, 0, 0, 0, 0, 48]
POOL_SHARE = [0, 192, 192, 192, 192, 192, 192, 0, 0]


def tile_picked_deform_lin_gelu_def_e_kernel(tc, xT, w, b, offs, out):
    nc = tc.nc
    with ExitStack() as ctx:
        keep = ctx.enter_context(tc.tile_pool(name="keep", bufs=1))
        loads = ctx.enter_context(tc.tile_pool(name="loads", bufs=1))
        psum = ctx.enter_context(tc.psum_pool(name="psum", bufs=1))

        lists = keep.tile([P, D * V // 16], U16, name="lists")
        words = keep.tile([P, T], U32, name="words", align_bytes=64)
        scales = keep.tile([P, T], U8, name="scales", align_bytes=64)
        bias = keep.tile([P, 1], F32, name="bias")
        nc.gpsimd.memset(scales[:].bitcast(I32), 0)

        starts = [sum(WIDTHS[:i]) for i in range(len(WIDTHS))]
        column_bytes = PACK * 4
        x_view = xT.rearrange("(p j) t -> p j t", j=PACK)
        raws = []
        for i, width in enumerate(WIDTHS):
            raw = loads.tile([P, PACK, width], F32, name="raw%d" % i, align_bytes=64, offset=starts[i] * column_bytes)
            nc.sync.dma_start(out=raw[:], in_=x_view[:, :, starts[i] : starts[i] + width])
            raws.append(raw)
            if i == 0:
                nc.sync.dma_start(lists[:], offs)
        w_raw, w_place = [], []
        for h in range(2):
            place = (T + 2 * N * h) * column_bytes
            wr = loads.tile([P, 2, PACK, N], F32, name="w_raw%d" % h, align_bytes=64, offset=place)
            nc.sync.dma_start(out=wr[:], in_=w[2 * h : 2 * h + 2].rearrange("d (p j) m -> p d j m", j=PACK))
            w_raw.append(wr)
            w_place.append(place)
        nc.sync.dma_start(out=bias[:], in_=b)

        def interleave(copy, run, dst, src):
            copy(
                out=dst.rearrange("p (c i) t -> p c t i", i=run),
                in_=src.rearrange("p t (c i) -> p c t i", i=run),
            )

        bases = [starts[i] - sum(POOL_SHARE[: i + 1]) for i in range(len(WIDTHS))]
        staged = keep.tile([P, T - sum(POOL_SHARE), PACK], BF16, name="staged", align_bytes=64)

        def quantise(i):
            width, raw, pool = WIDTHS[i], raws[i], POOL_SHARE[i]
            grouped = staged[:, bases[i] : bases[i] + width, :]
            own = width - VECTOR_SHARE[i]
            if pool:
                nc.gpsimd.tensor_copy(out=grouped[:, 0:pool, :], in_=raw[:, :, 0:pool].rearrange("p t c -> p c t"))
            interleave(nc.scalar.copy, 2, grouped[:, pool:own, :], raw[:, :, pool:own])
            if own < width:
                interleave(nc.vector.tensor_copy, 4, grouped[:, own:, :], raw[:, :, own:])
            cols = slice(starts[i], starts[i] + width)
            nc.vector.quantize_mx(
                out=words[:, cols].bitcast(FP8X4), scales=scales[:, cols], in_=grouped.rearrange("p c t -> p (c t)")
            )

        pieces = {(sort, t): [] for sort in "wb" for t in range(D)}

        def room(sort, t, lo, hi, place=None):
            dtype = U32 if sort == "w" else U8
            name = "%s%d_%d" % (sort, t, lo)
            if place is None:
                tile = keep.tile([P, hi - lo], dtype, name=name, align_bytes=64)
            else:
                tile = loads.tile([P, hi - lo], dtype, name=name, align_bytes=64, offset=place)
            pieces[(sort, t)].append((lo, hi, tile))
            return tile

        def part(sort, t, lo, hi):
            for a, z, tile in pieces[(sort, t)]:
                if a <= lo and hi <= z:
                    return tile[:, lo - a : hi - a]
            raise ValueError("no tile holds this range")

        def gather(sort, t, lo, hi, whole=False):
            table = words if sort == "w" else scales
            window = table[:] if whole else table[:, 0 : PACK * hi]
            nc.vector.tensor_copy(part(sort, t, lo, hi), window.indirect(lists[:, (t * V + lo) // 16 : (t * V + hi) // 16]))

        cut = HALF - EIGHTH
        for t in (0, 1):
            room("w", t, 0, HALF)
            room("w", t, HALF, HALF + QUARTER)
            room("b", t, HALF, V)
        for t in (2, 3):
            room("w", t, 0, HALF + QUARTER)
        room("b", 0, 0, HALF)
        room("b", 1, 0, QUARTER)
        for t in (2, 3):
            room("b", t, 0, EIGHTH)

        def held(t, lo, hi, i):
            room("b", t, lo, hi, starts[i] * column_bytes + t * QUARTER)
            gather("b", t, lo, hi)

        quantise(0)
        for sort in "wb":
            for t in range(D):
                gather(sort, t, 0, EIGHTH)
        quantise(1)
        for sort in "wb":
            for t in (0, 1):
                gather(sort, t, EIGHTH, QUARTER)
        quantise(2)
        for t in (2, 3):
            gather("w", t, EIGHTH, cut)
        quantise(3)
        for t in (0, 1):
            gather("w", t, QUARTER, HALF)
        gather("b", 0, QUARTER, HALF)
        quantise(4)
        for t in (1, 2, 3):
            held(t, QUARTER, HALF, 4)
        quantise(5)
        held(2, EIGHTH, QUARTER, 5)
        for t in (0, 1):
            gather("w", t, HALF, HALF + QUARTER, whole=True)
        for t in (2, 3):
            gather("w", t, cut, HALF + QUARTER)
        for i in (6, 7, 8):
            quantise(i)
        held(3, EIGHTH, QUARTER, 8)

        w_words = keep.tile([P, D * N], U32, name="w_words", align_bytes=64)
        w_scales = keep.tile([P, D * N], U8, name="w_scales", align_bytes=64)
        w_grouped = keep.tile([P, D, N, PACK], BF16, name="w_grouped", align_bytes=64)

        def quantise_w(h):
            for t in range(2 * h, 2 * h + 2):
                interleave(nc.scalar.copy, 2, w_grouped[:, t], w_raw[h][:, t % 2])
            cols = slice(2 * h * N, (2 * h + 2) * N)
            nc.vector.quantize_mx(
                out=w_words[:, cols].bitcast(FP8X4),
                scales=w_scales[:, cols],
                in_=w_grouped[:, 2 * h : 2 * h + 2].rearrange("p d m t -> p (d m t)"),
            )

        for t in (0, 1):
            gather("b", t, HALF, V)
        quantise_w(0)
        for t in (2, 3):
            room("b", t, HALF, V, w_place[0] + (t % 2) * HALF)
            gather("b", t, HALF, V)
        quantise_w(1)
        for t in range(D):
            room("w", t, HALF + QUARTER, V, w_place[1] + t * QUARTER * 4)
            gather("w", t, HALF + QUARTER, V)

        spans = [(0, HALF), (HALF, HALF + QUARTER), (HALF + QUARTER, V)]
        accs = [psum.tile([N, hi - lo], F32, name="acc%d" % g) for g, (lo, hi) in enumerate(spans)]

        def multiply(g, t):
            lo, hi = spans[g]
            edges = sorted({e for sort in "wb" for a, z, tile in pieces[(sort, t)] for e in (a, z) if lo <= e <= hi} | {lo, hi})
            cols = slice(t * N, (t + 1) * N)
            for a, z in zip(edges, edges[1:]):
                nc.tensor.matmul_mx(
                    out=accs[g][:, a - lo : z - lo],
                    lhsT=w_words[:, cols].bitcast(FP8X4),
                    lhsT_scale=w_scales[:, cols],
                    rhs=part("w", t, a, z).bitcast(FP8X4),
                    rhs_scale=part("b", t, a, z),
                    start=(t == 0 and a == lo),
                    stop=(t == D - 1 and z == hi),
                )

        def finish(g):
            lo, hi = spans[g]
            result = keep.tile([N, hi - lo], F32, name="result%d" % g)
            nc.scalar.activation(result[:], accs[g][:], GELU, bias=bias[:])
            nc.sync.dma_start(out=out[:, lo:hi], in_=result[:])

        for pair in ((0, 1), (2, 3)):
            for g in (0, 1):
                for t in pair:
                    multiply(g, t)
        for t in range(D):
            multiply(2, t)
        for g in range(len(spans)):
            finish(g)
